import numpy as np
import ml_dtypes


def mxq(x, axis, fmt="e4m3"):
    dtype, down = {"e4m3": (ml_dtypes.float8_e4m3fn, 7), "e5m2": (ml_dtypes.float8_e5m2, 14)}[fmt]
    v = np.moveaxis(np.asarray(x, np.float32).astype(ml_dtypes.bfloat16).astype(np.float64), axis, -1)
    blocks = v.reshape(v.shape[:-1] + (-1, 32))
    amax = np.abs(blocks).max(-1, keepdims=True)
    byte = np.maximum(np.where(amax > 0, np.frexp(amax)[1] - 1 + 127, 0) - down, 1)
    scale = np.exp2(byte - 127.0)
    codes = (blocks / scale).astype(np.float32).astype(dtype).astype(np.float64)
    return np.moveaxis((codes * scale).reshape(v.shape), -1, axis)


WIDE = False


def mx_kscale(k):
    if not WIDE:
        return np.ones(k)
    levels = np.array([10, -10, 5, -5, 0])
    if k % 512:
        return np.exp2(np.random.permutation(np.resize(levels, k // 32))).repeat(32)
    a = np.empty((k // 512, 16))
    for p in range(k // 512):
        a[p, :8] = np.random.permutation(np.resize(levels, 8))
        for g in range(8):
            far = levels[np.abs(levels - a[p, g]) >= 10]
            a[p, g + 8] = far[np.random.randint(len(far))]
    return np.exp2(a.ravel()).repeat(32)


BF16 = ml_dtypes.bfloat16


def bf(x):
    return np.asarray(x, np.float32).astype(BF16)


def f64(x):
    return np.asarray(x).astype(np.float64)


E2M1 = np.array([0.0, 0.5, 1.0, 1.5, 2.0, 3.0, 4.0, 6.0, -0.0, -0.5, -1.0, -1.5, -2.0, -3.0, -4.0, -6.0])


def pack_weight(w, fmt):
    k, n = w.shape
    w = f64(bf(w)).reshape(k // 32, 32, n)
    amax = np.abs(w).max(1)
    if fmt == "e4m3":
        byte = np.frexp(amax)[1] - 1 + 127 - 7
    else:
        mant, ex = np.frexp(amax / 6.0)
        byte = np.where(mant > 0.5, ex, ex - 1) + 127
    byte = np.clip(np.where(amax > 0, byte, 1), 1, 254)
    scaled = (w * np.exp2(127.0 - byte)[:, None, :]).reshape(k, n).astype(np.float32)
    by_word = np.ascontiguousarray(scaled.reshape(k // 512, 128, 4, n).transpose(0, 1, 3, 2))
    if fmt == "e4m3":
        words = by_word.astype(ml_dtypes.float8_e4m3fn).view(np.uint8)
    else:
        c = by_word.astype(ml_dtypes.float4_e2m1fn).view(np.uint8) & 0xF
        words = c[..., 0::2] | (c[..., 1::2] << 4)
    return np.ascontiguousarray(words), np.ascontiguousarray(byte.astype(np.uint8).reshape(k // 512, 16, n))


def unpack_weight(words, scales, fmt):
    g, p, n, _ = words.shape
    if fmt == "e4m3":
        vals = np.ascontiguousarray(words).view(ml_dtypes.float8_e4m3fn).astype(np.float64)
    else:
        nib = np.empty((g, p, n, 4), np.uint8)
        nib[..., 0::2] = words & 0xF
        nib[..., 1::2] = words >> 4
        vals = E2M1[nib]
    vals = vals * np.repeat(np.exp2(scales.astype(np.float64) - 127.0), 8, axis=1)[..., None]
    return vals.transpose(0, 1, 3, 2).reshape(g * 512, n)
def pack4(w):
    words, scales = pack_weight(w, "e2m1")
    return words.reshape(words.shape[0], 128, -1), scales


def unpack4(words, scales):
    return unpack_weight(words.reshape(words.shape[0], 128, -1, 2), scales, "e2m1")


M, K = 512, 1536

OMEGA = 0.25


def setup_inputs():
    s = mx_kscale(K)
    y = np.random.standard_normal((M, K)) * s
    r = np.random.standard_normal((K, K)) / np.sqrt(K) * (1 - np.eye(K))
    c = -OMEGA / (1 - OMEGA) * r / s[:, None] * s
    c_words, c_scales = pack4(c)
    back = (1 - OMEGA) ** 3 * (1 + 0.1 * np.random.standard_normal(K)) / s
    return {"y": bf(y),
            "c_words": c_words,
            "c_scales": c_scales,
            "back": bf(back)}


def reference(y, c_words, c_scales, back):
    c = unpack4(c_words, c_scales)
    y0 = f64(y)
    y1 = y0 + (mxq(y0, 1, "e4m3") @ c)
    y2 = y1 + (mxq(y1, 1, "e4m3") @ c)
    y3 = y2 + (mxq(y2, 1, "e4m3") @ c)
    return y3 * f64(back)

@@ -1,0 +1,202 @@
+from contextlib import ExitStack
+
+import concourse.mybir as mybir
+from concourse.masks import make_identity
+
+M, K = 512, 1536
+SWEEPS = 3
+FLOPS = SWEEPS * 2 * M * K * K
+
+F32 = mybir.dt.float32
+BF16 = mybir.dt.bfloat16
+I32 = mybir.dt.int32
+U32 = mybir.dt.uint32
+U8 = mybir.dt.uint8
+FP8X4 = mybir.dt.float8_e4m3fn_x4
+FP4X4 = mybir.dt.float4_e2m1fn_x4
+ADD = mybir.AluOpType.add
+MULT = mybir.AluOpType.mult
+
+P = 128
+CHUNK = 512
+GROUPS = K // CHUNK
+TILES = M // P
+WORDS = CHUNK // 2
+
+
+def tile_damped_jacobi_sweeps_t2_kernel(tc, y, c_words, c_scales, back, out):
+    nc = tc.nc
+
+    with ExitStack() as ctx:
+        keep = ctx.enter_context(tc.tile_pool(name="keep", bufs=1))
+        ring = ctx.enter_context(tc.tile_pool(name="ring", bufs=1))
+        psum = ctx.enter_context(tc.psum_pool(name="psum", bufs=1))
+        ctx.enter_context(tc.manual_schedule())
+
+        identity = keep.tile([P, P], F32, name="identity")
+        make_identity(nc, identity[:])
+
+        c_plane = keep.tile([P, GROUPS, K], U8, name="c_plane", align_bytes=64)
+        nc.vector.memset(c_plane[:].rearrange("p g n -> p (g n)").bitcast(I32), 0)
+
+        y_sb = [keep.tile([P, K], BF16, name="y_%d" % t, align_bytes=64) for t in range(TILES)]
+        c_sb = [keep.tile([P, 2 * K], U8, name="c_%d" % g, align_bytes=64) for g in range(GROUPS)]
+        back_sb = keep.tile([P, K], BF16, name="back_sb", align_bytes=64)
+
+        def load_y(t):
+            nc.sync.dma_start(out=y_sb[t][:], in_=y[t * P : (t + 1) * P, :])
+
+        def load_c(g):
+            nc.sync.dma_start(out=c_sb[g][:].bitcast(I32), in_=c_words[g].bitcast(I32))
+
+        load_y(0)
+        load_c(0)
+        for q in range(4):
+            nc.sync.dma_start(
+                out=c_plane[32 * q : 32 * q + 4, :, :].bitcast(I32),
+                in_=c_scales[:, 4 * q : 4 * q + 4, :].bitcast(I32).rearrange("g r n -> r g n"),
+            )
+        load_y(1)
+        load_c(1)
+        load_c(2)
+        load_y(2)
+        load_y(3)
+        nc.sync.dma_start(out=back_sb[:], in_=back.partition_broadcast(P))
+
+        state = {(t, g): y_sb[t][:, g * CHUNK : (g + 1) * CHUNK] for t in range(TILES) for g in range(GROUPS)}
+        sorted_words = {}
+        operand = {}
+        waiting_quantize = []
+        waiting_finish = []
+
+        def sort_y(t, groups):
+            n = len(groups)
+            words = keep.tile([P, n * WORDS], F32, name="ys_%d_%d" % (t, groups[0]), align_bytes=64)
+            src = y_sb[t][:].bitcast(F32)[:, groups[0] * WORDS : (groups[0] + n) * WORDS]
+            nc.vector.tensor_copy(
+                out=words[:].rearrange("p (g u j) -> p g u j", g=n, u=2),
+                in_=src.rearrange("p (g j u) -> p g u j", g=n, u=2),
+            )
+            for i, g in enumerate(groups):
+                sorted_words[t, g] = words[:, i * WORDS : (i + 1) * WORDS]
+
+        def transpose_run(sweep, bank_chunks):
+            banks = []
+            for chunks in bank_chunks:
+                bank = psum.tile([P, CHUNK], F32, name="turned", bufs=3)
+                for i, chunk in enumerate(chunks):
+                    for u in range(2):
+                        nc.tensor.transpose(
+                            bank[:, (2 * i + u) * P : (2 * i + u + 1) * P],
+                            sorted_words[chunk][:, u * P : (u + 1) * P],
+                            identity[:],
+                        )
+                banks.append(bank)
+            for chunks, bank in zip(bank_chunks, banks):
+                n = len(chunks)
+                grouped = ring.tile([P, n * WORDS], F32, name="grouped", bufs=4, align_bytes=64)
+                nc.scalar.copy(
+                    out=grouped[:].rearrange("p (c r u) -> p c r u", c=n, u=2),
+                    in_=bank[:, : n * WORDS].rearrange("p (c u r) -> p c r u", c=n, u=2),
+                )
+                waiting_quantize.append((sweep, chunks, grouped))
+
+        def quantize(count):
+            for sweep, chunks, grouped in waiting_quantize[:count]:
+                n = len(chunks)
+                name = "%d_%d_%d" % (sweep, chunks[0][0], chunks[0][1])
+                codes = keep.tile([P, n * P], U32, name="codes_" + name, align_bytes=64)
+                scales = keep.tile([P, n * P], U8, name="scales_" + name, align_bytes=64)
+                nc.vector.quantize_mx(out=codes[:].bitcast(FP8X4), scales=scales[:], in_=grouped[:].bitcast(BF16))
+                for i, chunk in enumerate(chunks):
+                    operand[chunk] = (codes[:, i * P : (i + 1) * P], scales[:, i * P : (i + 1) * P])
+            waiting_quantize[:count] = []
+
+        def mx_pass(acc, t, b, g):
+            codes, scales = operand[t, g]
+            nc.tensor.matmul_mx(
+                out=acc[:],
+                lhsT=codes.bitcast(FP8X4),
+                lhsT_scale=scales,
+                rhs=c_sb[g][:, 2 * b * CHUNK : 2 * (b + 1) * CHUNK].bitcast(FP4X4),
+                rhs_scale=c_plane[:, g, b * CHUNK : (b + 1) * CHUNK],
+                start=(g == 0),
+                stop=(g == GROUPS - 1),
+            )
+
+        def finish():
+            for t, b, total in waiting_finish:
+                cols = slice(b * CHUNK, (b + 1) * CHUNK)
+                result = ring.tile([P, CHUNK], F32, name="result", bufs=6)
+                nc.vector.tensor_tensor(out=result[:], in0=total[:], in1=back_sb[:, cols], op=MULT)
+                nc.sync.dma_start(out=out[t * P : (t + 1) * P, cols], in_=result[:])
+            waiting_finish.clear()
+
+        def drain(sweep, t, b, acc):
+            if sweep < SWEEPS:
+                new = keep.tile([P, CHUNK], F32, name="state_%d_%d_%d" % (sweep, t, b))
+            else:
+                new = ring.tile([P, CHUNK], F32, name="total", bufs=4)
+            nc.vector.tensor_tensor(out=new[:], in0=acc[:], in1=state[t, b], op=ADD)
+            quantize(len(waiting_quantize))
+            if sweep < SWEEPS:
+                state[t, b] = new[:]
+                rounded = ring.tile([P, CHUNK], BF16, name="rounded", bufs=12, align_bytes=64)
+                nc.scalar.copy(
+                    out=rounded[:].rearrange("p (u j e) -> p u j e", u=2, e=2),
+                    in_=new[:].rearrange("p (j u e) -> p u j e", u=2, e=2),
+                )
+                sorted_words[t, b] = rounded[:].bitcast(F32)
+            else:
+                finish()
+                waiting_finish.append((t, b, new))
+
+        def new_acc():
+            return psum.tile([P, CHUNK], F32, name="acc", bufs=5)
+
+        def multiply(sweep, t, banks):
+            for b in banks:
+                acc = new_acc()
+                for g in range(GROUPS):
+                    mx_pass(acc, t, b, g)
+                drain(sweep, t, b, acc)
+
+        def turn_pair(sweep, first):
+            chunks = [(t, g) for t in (first, first + 1) for g in range(GROUPS)]
+            transpose_run(sweep, [chunks[i : i + 2] for i in range(0, len(chunks), 2)])
+            quantize(1)
+
+        every_bank = range(GROUPS)
+
+        for g in range(GROUPS):
+            sort_y(0, [g])
+        transpose_run(1, [[(0, g)] for g in range(GROUPS)])
+        quantize(GROUPS)
+        sort_y(1, [0, 1, 2])
+        accs = [new_acc() for b in every_bank]
+        for b in every_bank:
+            mx_pass(accs[b], 0, b, 0)
+        transpose_run(1, [[(1, 0), (1, 1)], [(1, 2)]])
+        quantize(2)
+        for g in range(1, GROUPS):
+            for b in every_bank:
+                mx_pass(accs[b], 0, b, g)
+        sort_y(2, [0, 1, 2])
+        drain(1, 0, 0, accs[0])
+        sort_y(3, [0, 1, 2])
+        drain(1, 0, 1, accs[1])
+        drain(1, 0, 2, accs[2])
+        multiply(1, 1, [0])
+        turn_pair(1, 2)
+        multiply(1, 1, [1, 2])
+        multiply(1, 2, every_bank)
+
+        for sweep in range(2, SWEEPS + 1):
+            turn_pair(sweep, 0)
+            multiply(sweep - 1, 3, every_bank)
+            multiply(sweep, 0, every_bank)
+            turn_pair(sweep, 2)
+            multiply(sweep, 1, every_bank)
+            multiply(sweep, 2, every_bank)
+        multiply(SWEEPS, 3, every_bank)
+        finish()

@@ -36,8 +36,11 @@ def tile_damped_jacobi_sweeps_t2_kernel(tc, y, c_words, c_scales, back, out):
         identity = keep.tile([P, P], F32, name="identity")
         make_identity(nc, identity[:])
 
-        c_plane = keep.tile([P, GROUPS, K], U8, name="c_plane", align_bytes=64)
-        nc.vector.memset(c_plane[:].rearrange("p g n -> p (g n)").bitcast(I32), 0)
+        plane_first = keep.tile([P, 1, K], U8, name="plane_first", align_bytes=64)
+        plane_rest = keep.tile([P, GROUPS - 1, K], U8, name="plane_rest", align_bytes=64)
+        for plane in (plane_first, plane_rest):
+            nc.vector.memset(plane[:].rearrange("p g n -> p (g n)").bitcast(I32), 0)
+        c_plane = [plane_first[:, 0, :]] + [plane_rest[:, i, :] for i in range(GROUPS - 1)]
 
         y_sb = [keep.tile([P, K], BF16, name="y_%d" % t, align_bytes=64) for t in range(TILES)]
         c_sb = [keep.tile([P, 2 * K], U8, name="c_%d" % g, align_bytes=64) for g in range(GROUPS)]
@@ -49,14 +52,18 @@ def tile_damped_jacobi_sweeps_t2_kernel(tc, y, c_words, c_scales, back, out):
         def load_c(g):
             nc.sync.dma_start(out=c_sb[g][:].bitcast(I32), in_=c_words[g].bitcast(I32))
 
+        def load_scales(plane, groups):
+            for q in range(4):
+                nc.sync.dma_start(
+                    out=plane[32 * q : 32 * q + 4, :, :].bitcast(I32),
+                    in_=c_scales[groups, 4 * q : 4 * q + 4, :].bitcast(I32).rearrange("g r n -> r g n"),
+                )
+
         load_y(0)
+        load_scales(plane_first, slice(0, 1))
         load_c(0)
-        for q in range(4):
-            nc.sync.dma_start(
-                out=c_plane[32 * q : 32 * q + 4, :, :].bitcast(I32),
-                in_=c_scales[:, 4 * q : 4 * q + 4, :].bitcast(I32).rearrange("g r n -> r g n"),
-            )
         load_y(1)
+        load_scales(plane_rest, slice(1, GROUPS))
         load_c(1)
         load_c(2)
         load_y(2)
@@ -68,6 +75,7 @@ def tile_damped_jacobi_sweeps_t2_kernel(tc, y, c_words, c_scales, back, out):
         operand = {}
         waiting_quantize = []
         waiting_finish = []
+        waiting_round = []
 
         def sort_y(t, groups):
             n = len(groups)
@@ -119,7 +127,7 @@ def tile_damped_jacobi_sweeps_t2_kernel(tc, y, c_words, c_scales, back, out):
                 lhsT=codes.bitcast(FP8X4),
                 lhsT_scale=scales,
                 rhs=c_sb[g][:, 2 * b * CHUNK : 2 * (b + 1) * CHUNK].bitcast(FP4X4),
-                rhs_scale=c_plane[:, g, b * CHUNK : (b + 1) * CHUNK],
+                rhs_scale=c_plane[g][:, b * CHUNK : (b + 1) * CHUNK],
                 start=(g == 0),
                 stop=(g == GROUPS - 1),
             )
@@ -132,39 +140,44 @@ def tile_damped_jacobi_sweeps_t2_kernel(tc, y, c_words, c_scales, back, out):
                 nc.sync.dma_start(out=out[t * P : (t + 1) * P, cols], in_=result[:])
             waiting_finish.clear()
 
-        def drain(sweep, t, b, acc):
+        def add_residual(sweep, t, b, acc):
             if sweep < SWEEPS:
                 new = keep.tile([P, CHUNK], F32, name="state_%d_%d_%d" % (sweep, t, b))
             else:
                 new = ring.tile([P, CHUNK], F32, name="total", bufs=4)
             nc.vector.tensor_tensor(out=new[:], in0=acc[:], in1=state[t, b], op=ADD)
+            state[t, b] = new[:]
+            finish()
             quantize(len(waiting_quantize))
-            if sweep < SWEEPS:
-                state[t, b] = new[:]
+            (waiting_finish if sweep == SWEEPS else waiting_round).append((t, b, new))
+
+        def round_states():
+            for t, b, new in waiting_round:
                 rounded = ring.tile([P, CHUNK], BF16, name="rounded", bufs=12, align_bytes=64)
                 nc.scalar.copy(
                     out=rounded[:].rearrange("p (u j e) -> p u j e", u=2, e=2),
                     in_=new[:].rearrange("p (j u e) -> p u j e", u=2, e=2),
                 )
                 sorted_words[t, b] = rounded[:].bitcast(F32)
-            else:
-                finish()
-                waiting_finish.append((t, b, new))
+            waiting_round.clear()
 
         def new_acc():
             return psum.tile([P, CHUNK], F32, name="acc", bufs=5)
 
-        def multiply(sweep, t, banks):
-            for b in banks:
+        def turn(*jobs):
+            chunks = [(t, g) for sweep, t in jobs for g in range(GROUPS)]
+            transpose_run(jobs[0][0], [chunks[i : i + 2] for i in range(0, len(chunks), 2)])
+            quantize(2)
+
+        def multiply(sweep, t, jobs=(), after_bank=1):
+            for b in range(GROUPS):
                 acc = new_acc()
                 for g in range(GROUPS):
                     mx_pass(acc, t, b, g)
-                drain(sweep, t, b, acc)
-
-        def turn_pair(sweep, first):
-            chunks = [(t, g) for t in (first, first + 1) for g in range(GROUPS)]
-            transpose_run(sweep, [chunks[i : i + 2] for i in range(0, len(chunks), 2)])
-            quantize(1)
+                add_residual(sweep, t, b, acc)
+                if jobs and b == after_bank:
+                    turn(*jobs)
+                round_states()
 
         every_bank = range(GROUPS)
 
@@ -182,21 +195,19 @@ def tile_damped_jacobi_sweeps_t2_kernel(tc, y, c_words, c_scales, back, out):
             for b in every_bank:
                 mx_pass(accs[b], 0, b, g)
         sort_y(2, [0, 1, 2])
-        drain(1, 0, 0, accs[0])
+        for b in every_bank:
+            round_states()
+            add_residual(1, 0, b, accs[b])
+        multiply(1, 1, [(1, 2)], after_bank=0)
         sort_y(3, [0, 1, 2])
-        drain(1, 0, 1, accs[1])
-        drain(1, 0, 2, accs[2])
-        multiply(1, 1, [0])
-        turn_pair(1, 2)
-        multiply(1, 1, [1, 2])
-        multiply(1, 2, every_bank)
-
-        for sweep in range(2, SWEEPS + 1):
-            turn_pair(sweep, 0)
-            multiply(sweep - 1, 3, every_bank)
-            multiply(sweep, 0, every_bank)
-            turn_pair(sweep, 2)
-            multiply(sweep, 1, every_bank)
-            multiply(sweep, 2, every_bank)
-        multiply(SWEEPS, 3, every_bank)
+        multiply(1, 2, [(2, 0), (2, 1)])
+        multiply(2, 0)
+        multiply(2, 1, [(1, 3), (2, 2)])
+        multiply(1, 3, [(3, 0), (3, 1)])
+        multiply(3, 0)
+        multiply(2, 2)
+        multiply(3, 1, [(2, 3), (3, 2)])
+        multiply(2, 3)
+        multiply(3, 2, [(3, 3)])
+        multiply(3, 3)
         finish()

@@ -21,7 +21,16 @@ P = 128
 CHUNK = 512
 GROUPS = K // CHUNK
 TILES = M // P
-WORDS = CHUNK // 2
+PAIRS = CHUNK // 2
+PASSES = GROUPS * GROUPS
+QUADRANTS = 4
+
+TURN_BANKS = 3
+SUM_BANKS = 8 - TURN_BANKS
+
+GPSIMD_COLUMNS = 192
+
+FIRST_TURN_AFTER = 4
 
 
 def tile_damped_jacobi_sweeps_t2_kernel(tc, y, c_words, c_scales, back, out):
@@ -36,11 +45,11 @@ def tile_damped_jacobi_sweeps_t2_kernel(tc, y, c_words, c_scales, back, out):
         identity = keep.tile([P, P], F32, name="identity")
         make_identity(nc, identity[:])
 
-        plane_first = keep.tile([P, 1, K], U8, name="plane_first", align_bytes=64)
-        plane_rest = keep.tile([P, GROUPS - 1, K], U8, name="plane_rest", align_bytes=64)
-        for plane in (plane_first, plane_rest):
-            nc.vector.memset(plane[:].rearrange("p g n -> p (g n)").bitcast(I32), 0)
-        c_plane = [plane_first[:, 0, :]] + [plane_rest[:, i, :] for i in range(GROUPS - 1)]
+        scales_first = keep.tile([P, 1, K], U8, name="scales_first", align_bytes=64)
+        scales_rest = keep.tile([P, GROUPS - 1, K], U8, name="scales_rest", align_bytes=64)
+        for scale_tile in (scales_first, scales_rest):
+            nc.vector.memset(scale_tile[:].rearrange("p g n -> p (g n)").bitcast(I32), 0)
+        c_scale_sb = [scales_first[:, 0, :]] + [scales_rest[:, i, :] for i in range(GROUPS - 1)]
 
         y_sb = [keep.tile([P, K], BF16, name="y_%d" % t, align_bytes=64) for t in range(TILES)]
         c_sb = [keep.tile([P, 2 * K], U8, name="c_%d" % g, align_bytes=64) for g in range(GROUPS)]
@@ -52,65 +61,74 @@ def tile_damped_jacobi_sweeps_t2_kernel(tc, y, c_words, c_scales, back, out):
         def load_c(g):
             nc.sync.dma_start(out=c_sb[g][:].bitcast(I32), in_=c_words[g].bitcast(I32))
 
-        def load_scales(plane, groups):
-            for q in range(4):
+        def load_scales(scale_tile, groups):
+            for q in range(QUADRANTS):
                 nc.sync.dma_start(
-                    out=plane[32 * q : 32 * q + 4, :, :].bitcast(I32),
+                    out=scale_tile[32 * q : 32 * q + 4, :, :].bitcast(I32),
                     in_=c_scales[groups, 4 * q : 4 * q + 4, :].bitcast(I32).rearrange("g r n -> r g n"),
                 )
 
         load_y(0)
-        load_scales(plane_first, slice(0, 1))
-        load_c(0)
         load_y(1)
-        load_scales(plane_rest, slice(1, GROUPS))
+        load_scales(scales_first, slice(0, 1))
+        load_c(0)
+        load_scales(scales_rest, slice(1, GROUPS))
         load_c(1)
         load_c(2)
         load_y(2)
         load_y(3)
-        nc.sync.dma_start(out=back_sb[:], in_=back.partition_broadcast(P))
 
         state = {(t, g): y_sb[t][:, g * CHUNK : (g + 1) * CHUNK] for t in range(TILES) for g in range(GROUPS)}
-        sorted_words = {}
+        sorted_pairs = {}
         operand = {}
-        waiting_quantize = []
-        waiting_finish = []
-        waiting_round = []
+        to_round = []
+        to_quantize = []
+        to_finish = []
 
-        def sort_y(t, groups):
+        def sort_y(t, groups, copy):
             n = len(groups)
-            words = keep.tile([P, n * WORDS], F32, name="ys_%d_%d" % (t, groups[0]), align_bytes=64)
-            src = y_sb[t][:].bitcast(F32)[:, groups[0] * WORDS : (groups[0] + n) * WORDS]
-            nc.vector.tensor_copy(
-                out=words[:].rearrange("p (g u j) -> p g u j", g=n, u=2),
-                in_=src.rearrange("p (g j u) -> p g u j", g=n, u=2),
+            pairs = keep.tile([P, n * PAIRS], F32, name="y_pairs_%d_%d" % (t, groups[0]), align_bytes=64)
+            source = y_sb[t][:].bitcast(F32)[:, groups[0] * PAIRS : (groups[0] + n) * PAIRS]
+            copy(
+                out=pairs[:].rearrange("p (g u j) -> p g u j", g=n, u=2),
+                in_=source.rearrange("p (g j u) -> p g u j", g=n, u=2),
             )
             for i, g in enumerate(groups):
-                sorted_words[t, g] = words[:, i * WORDS : (i + 1) * WORDS]
+                sorted_pairs[t, g] = pairs[:, i * PAIRS : (i + 1) * PAIRS]
 
-        def transpose_run(sweep, bank_chunks):
+        def round_states():
+            for t, g in to_round:
+                rounded = ring.tile([P, CHUNK], BF16, name="rounded", bufs=TILES * GROUPS, align_bytes=64)
+                nc.scalar.copy(
+                    out=rounded[:].rearrange("p (u j e) -> p u j e", u=2, e=2),
+                    in_=state[t, g].rearrange("p (j u e) -> p u j e", u=2, e=2),
+                )
+                sorted_pairs[t, g] = rounded[:].bitcast(F32)
+            to_round.clear()
+
+        def turn(sweep, chunks_by_bank):
             banks = []
-            for chunks in bank_chunks:
-                bank = psum.tile([P, CHUNK], F32, name="turned", bufs=3)
+            for chunks in chunks_by_bank:
+                bank = psum.tile([P, CHUNK], F32, name="turned", bufs=TURN_BANKS)
                 for i, chunk in enumerate(chunks):
                     for u in range(2):
                         nc.tensor.transpose(
                             bank[:, (2 * i + u) * P : (2 * i + u + 1) * P],
-                            sorted_words[chunk][:, u * P : (u + 1) * P],
+                            sorted_pairs[chunk][:, u * P : (u + 1) * P],
                             identity[:],
                         )
                 banks.append(bank)
-            for chunks, bank in zip(bank_chunks, banks):
+            for chunks, bank in zip(chunks_by_bank, banks):
                 n = len(chunks)
-                grouped = ring.tile([P, n * WORDS], F32, name="grouped", bufs=4, align_bytes=64)
+                grouped = ring.tile([P, n * PAIRS], F32, name="grouped", bufs=TURN_BANKS + 1, align_bytes=64)
                 nc.scalar.copy(
                     out=grouped[:].rearrange("p (c r u) -> p c r u", c=n, u=2),
-                    in_=bank[:, : n * WORDS].rearrange("p (c u r) -> p c r u", c=n, u=2),
+                    in_=bank[:, : n * PAIRS].rearrange("p (c u r) -> p c r u", c=n, u=2),
                 )
-                waiting_quantize.append((sweep, chunks, grouped))
+                to_quantize.append((sweep, chunks, grouped))
 
         def quantize(count):
-            for sweep, chunks, grouped in waiting_quantize[:count]:
+            for sweep, chunks, grouped in to_quantize[:count]:
                 n = len(chunks)
                 name = "%d_%d_%d" % (sweep, chunks[0][0], chunks[0][1])
                 codes = keep.tile([P, n * P], U32, name="codes_" + name, align_bytes=64)
@@ -118,96 +136,105 @@ def tile_damped_jacobi_sweeps_t2_kernel(tc, y, c_words, c_scales, back, out):
                 nc.vector.quantize_mx(out=codes[:].bitcast(FP8X4), scales=scales[:], in_=grouped[:].bitcast(BF16))
                 for i, chunk in enumerate(chunks):
                     operand[chunk] = (codes[:, i * P : (i + 1) * P], scales[:, i * P : (i + 1) * P])
-            waiting_quantize[:count] = []
+            to_quantize[:count] = []
 
-        def mx_pass(acc, t, b, g):
+        def turn_tile_pair(sweep, first):
+            chunks = [(t, g) for t in (first, first + 1) for g in range(GROUPS)]
+            turn(sweep, [chunks[i : i + 2] for i in range(0, len(chunks), 2)])
+            quantize(2)
+
+        def new_sum_bank():
+            return psum.tile([P, CHUNK], F32, name="sums", bufs=SUM_BANKS)
+
+        def mx_pass(sums, t, b, g):
             codes, scales = operand[t, g]
             nc.tensor.matmul_mx(
-                out=acc[:],
+                out=sums[:],
                 lhsT=codes.bitcast(FP8X4),
                 lhsT_scale=scales,
                 rhs=c_sb[g][:, 2 * b * CHUNK : 2 * (b + 1) * CHUNK].bitcast(FP4X4),
-                rhs_scale=c_plane[g][:, b * CHUNK : (b + 1) * CHUNK],
+                rhs_scale=c_scale_sb[g][:, b * CHUNK : (b + 1) * CHUNK],
                 start=(g == 0),
                 stop=(g == GROUPS - 1),
             )
 
-        def finish():
-            for t, b, total in waiting_finish:
-                cols = slice(b * CHUNK, (b + 1) * CHUNK)
-                result = ring.tile([P, CHUNK], F32, name="result", bufs=6)
-                nc.vector.tensor_tensor(out=result[:], in0=total[:], in1=back_sb[:, cols], op=MULT)
-                nc.sync.dma_start(out=out[t * P : (t + 1) * P, cols], in_=result[:])
-            waiting_finish.clear()
+        def new_result():
+            return ring.tile([P, CHUNK], F32, name="result", bufs=6)
 
-        def add_residual(sweep, t, b, acc):
+        def times_back(engine, t, b, result, first, last):
+            engine.tensor_tensor(
+                out=result[:, first:last],
+                in0=state[t, b][:, first:last],
+                in1=back_sb[:, b * CHUNK + first : b * CHUNK + last],
+                op=MULT,
+            )
+
+        def store(t, b, result, first, last):
+            nc.sync.dma_start(
+                out=out[t * P : (t + 1) * P, b * CHUNK + first : b * CHUNK + last], in_=result[:, first:last]
+            )
+
+        def add_residual(sweep, t, b, sums):
             if sweep < SWEEPS:
                 new = keep.tile([P, CHUNK], F32, name="state_%d_%d_%d" % (sweep, t, b))
+                to_round.append((t, b))
             else:
                 new = ring.tile([P, CHUNK], F32, name="total", bufs=4)
-            nc.vector.tensor_tensor(out=new[:], in0=acc[:], in1=state[t, b], op=ADD)
+            nc.vector.tensor_tensor(out=new[:], in0=sums[:], in1=state[t, b], op=ADD)
             state[t, b] = new[:]
-            finish()
-            quantize(len(waiting_quantize))
-            (waiting_finish if sweep == SWEEPS else waiting_round).append((t, b, new))
+            for earlier_t, earlier_b, result in to_finish:
+                times_back(nc.vector, earlier_t, earlier_b, result, GPSIMD_COLUMNS, CHUNK)
+                store(earlier_t, earlier_b, result, 0, CHUNK)
+            to_finish.clear()
+            quantize(len(to_quantize))
 
-        def round_states():
-            for t, b, new in waiting_round:
-                rounded = ring.tile([P, CHUNK], BF16, name="rounded", bufs=12, align_bytes=64)
-                nc.scalar.copy(
-                    out=rounded[:].rearrange("p (u j e) -> p u j e", u=2, e=2),
-                    in_=new[:].rearrange("p (j u e) -> p u j e", u=2, e=2),
-                )
-                sorted_words[t, b] = rounded[:].bitcast(F32)
-            waiting_round.clear()
-
-        def new_acc():
-            return psum.tile([P, CHUNK], F32, name="acc", bufs=5)
-
-        def turn(*jobs):
-            chunks = [(t, g) for sweep, t in jobs for g in range(GROUPS)]
-            transpose_run(jobs[0][0], [chunks[i : i + 2] for i in range(0, len(chunks), 2)])
-            quantize(2)
-
-        def multiply(sweep, t, jobs=(), after_bank=1):
+        def sweep_tile(sweep, t, pair=None, turn_after=PASSES):
             for b in range(GROUPS):
-                acc = new_acc()
+                sums = new_sum_bank()
                 for g in range(GROUPS):
-                    mx_pass(acc, t, b, g)
-                add_residual(sweep, t, b, acc)
-                if jobs and b == after_bank:
-                    turn(*jobs)
-                round_states()
+                    mx_pass(sums, t, b, g)
+                    if g == GROUPS - 1:
+                        add_residual(sweep, t, b, sums)
+                        if sweep == SWEEPS and (t, b) != (TILES - 1, GROUPS - 1):
+                            result = new_result()
+                            times_back(nc.gpsimd, t, b, result, 0, GPSIMD_COLUMNS)
+                            to_finish.append((t, b, result))
+                    if pair and b * GROUPS + g + 1 == turn_after:
+                        turn_tile_pair(*pair)
+                if not pair or (b + 1) * GROUPS >= turn_after:
+                    round_states()
 
-        every_bank = range(GROUPS)
+        all_groups = list(range(GROUPS))
 
-        for g in range(GROUPS):
-            sort_y(0, [g])
-        transpose_run(1, [[(0, g)] for g in range(GROUPS)])
+        for g in all_groups:
+            sort_y(0, [g], nc.vector.tensor_copy)
+        turn(1, [[(0, g)] for g in all_groups])
+        sort_y(1, all_groups, nc.vector.tensor_copy)
         quantize(GROUPS)
-        sort_y(1, [0, 1, 2])
-        accs = [new_acc() for b in every_bank]
-        for b in every_bank:
-            mx_pass(accs[b], 0, b, 0)
-        transpose_run(1, [[(1, 0), (1, 1)], [(1, 2)]])
+        turn(1, [[(1, 0), (1, 1)], [(1, 2)]])
         quantize(2)
-        for g in range(1, GROUPS):
-            for b in every_bank:
-                mx_pass(accs[b], 0, b, g)
-        sort_y(2, [0, 1, 2])
-        for b in every_bank:
+
+        first_sums = [new_sum_bank() for b in all_groups]
+        for g in all_groups:
+            for b in all_groups:
+                mx_pass(first_sums[b], 0, b, g)
+        sort_y(2, all_groups, nc.scalar.copy)
+        sort_y(3, all_groups, nc.scalar.copy)
+        for b in all_groups:
             round_states()
-            add_residual(1, 0, b, accs[b])
-        multiply(1, 1, [(1, 2)], after_bank=0)
-        sort_y(3, [0, 1, 2])
-        multiply(1, 2, [(2, 0), (2, 1)])
-        multiply(2, 0)
-        multiply(2, 1, [(1, 3), (2, 2)])
-        multiply(1, 3, [(3, 0), (3, 1)])
-        multiply(3, 0)
-        multiply(2, 2)
-        multiply(3, 1, [(2, 3), (3, 2)])
-        multiply(2, 3)
-        multiply(3, 2, [(3, 3)])
-        multiply(3, 3)
-        finish()
+            add_residual(1, 0, b, first_sums[b])
+        sweep_tile(1, 1, (1, 2), FIRST_TURN_AFTER)
+        sweep_tile(1, 2, (2, 0))
+        nc.scalar.dma_start(out=back_sb[:], in_=back.partition_broadcast(P))
+        sweep_tile(1, 3)
+
+        for sweep in range(2, SWEEPS + 1):
+            sweep_tile(sweep, 0, (sweep, 2))
+            sweep_tile(sweep, 1)
+            sweep_tile(sweep, 2, (sweep + 1, 0) if sweep < SWEEPS else None)
+            sweep_tile(sweep, 3)
+
+        for first in (0, CHUNK // 2):
+            result = new_result()
+            times_back(nc.vector, TILES - 1, GROUPS - 1, result, first, first + CHUNK // 2)
+            store(TILES - 1, GROUPS - 1, result, first, first + CHUNK // 2)

@@ -55,8 +55,8 @@ def tile_damped_jacobi_sweeps_t2_kernel(tc, y, c_words, c_scales, back, out):
         c_sb = [keep.tile([P, 2 * K], U8, name="c_%d" % g, align_bytes=64) for g in range(GROUPS)]
         back_sb = keep.tile([P, K], BF16, name="back_sb", align_bytes=64)
 
-        def load_y(t):
-            nc.sync.dma_start(out=y_sb[t][:], in_=y[t * P : (t + 1) * P, :])
+        def load_y(t, first=0, last=K):
+            nc.sync.dma_start(out=y_sb[t][:, first:last], in_=y[t * P : (t + 1) * P, first:last])
 
         def load_c(g):
             nc.sync.dma_start(out=c_sb[g][:].bitcast(I32), in_=c_words[g].bitcast(I32))
@@ -68,7 +68,8 @@ def tile_damped_jacobi_sweeps_t2_kernel(tc, y, c_words, c_scales, back, out):
                     in_=c_scales[groups, 4 * q : 4 * q + 4, :].bitcast(I32).rearrange("g r n -> r g n"),
                 )
 
-        load_y(0)
+        load_y(0, 0, CHUNK)
+        load_y(0, CHUNK, K)
         load_y(1)
         load_scales(scales_first, slice(0, 1))
         load_c(0)
@@ -188,6 +189,21 @@ def tile_damped_jacobi_sweeps_t2_kernel(tc, y, c_words, c_scales, back, out):
             to_finish.clear()
             quantize(len(to_quantize))
 
+        def begin_product(t, b, transposes_follow):
+            if (t, b) == (TILES - 1, GROUPS - 1):
+                for first in (0, CHUNK // 2):
+                    result = new_result()
+                    times_back(nc.vector, t, b, result, first, first + CHUNK // 2)
+                    store(t, b, result, first, first + CHUNK // 2)
+            elif transposes_follow:
+                result = new_result()
+                times_back(nc.vector, t, b, result, 0, CHUNK)
+                store(t, b, result, 0, CHUNK)
+            else:
+                result = new_result()
+                times_back(nc.gpsimd, t, b, result, 0, GPSIMD_COLUMNS)
+                to_finish.append((t, b, result))
+
         def sweep_tile(sweep, t, pair=None, turn_after=PASSES):
             for b in range(GROUPS):
                 sums = new_sum_bank()
@@ -195,10 +211,8 @@ def tile_damped_jacobi_sweeps_t2_kernel(tc, y, c_words, c_scales, back, out):
                     mx_pass(sums, t, b, g)
                     if g == GROUPS - 1:
                         add_residual(sweep, t, b, sums)
-                        if sweep == SWEEPS and (t, b) != (TILES - 1, GROUPS - 1):
-                            result = new_result()
-                            times_back(nc.gpsimd, t, b, result, 0, GPSIMD_COLUMNS)
-                            to_finish.append((t, b, result))
+                        if sweep == SWEEPS:
+                            begin_product(t, b, bool(pair) and b == GROUPS - 1)
                     if pair and b * GROUPS + g + 1 == turn_after:
                         turn_tile_pair(*pair)
                 if not pair or (b + 1) * GROUPS >= turn_after:
@@ -209,7 +223,8 @@ def tile_damped_jacobi_sweeps_t2_kernel(tc, y, c_words, c_scales, back, out):
         for g in all_groups:
             sort_y(0, [g], nc.vector.tensor_copy)
         turn(1, [[(0, g)] for g in all_groups])
-        sort_y(1, all_groups, nc.vector.tensor_copy)
+        for g in all_groups:
+            sort_y(1, [g], nc.vector.tensor_copy)
         quantize(GROUPS)
         turn(1, [[(1, 0), (1, 1)], [(1, 2)]])
         quantize(2)
@@ -233,8 +248,3 @@ def tile_damped_jacobi_sweeps_t2_kernel(tc, y, c_words, c_scales, back, out):
             sweep_tile(sweep, 1)
             sweep_tile(sweep, 2, (sweep + 1, 0) if sweep < SWEEPS else None)
             sweep_tile(sweep, 3)
-
-        for first in (0, CHUNK // 2):
-            result = new_result()
-            times_back(nc.vector, TILES - 1, GROUPS - 1, result, first, first + CHUNK // 2)
-            store(TILES - 1, GROUPS - 1, result, first, first + CHUNK // 2)

from contextlib import ExitStack

import concourse.mybir as mybir
from concourse.masks import make_identity

M, K = 512, 1536
SWEEPS = 3
FLOPS = SWEEPS * 2 * M * K * K

F32 = mybir.dt.float32
BF16 = mybir.dt.bfloat16
I32 = mybir.dt.int32
U32 = mybir.dt.uint32
U8 = mybir.dt.uint8
FP8X4 = mybir.dt.float8_e4m3fn_x4
FP4X4 = mybir.dt.float4_e2m1fn_x4
ADD = mybir.AluOpType.add
MULT = mybir.AluOpType.mult

P = 128
CHUNK = 512
GROUPS = K // CHUNK
TILES = M // P
PAIRS = CHUNK // 2
PASSES = GROUPS * GROUPS
QUADRANTS = 4

TURN_BANKS = 3
SUM_BANKS = 8 - TURN_BANKS

GPSIMD_COLUMNS = 192

FIRST_TURN_AFTER = 4


def tile_damped_jacobi_sweeps_t2_kernel(tc, y, c_words, c_scales, back, out):
    nc = tc.nc

    with ExitStack() as ctx:
        keep = ctx.enter_context(tc.tile_pool(name="keep", bufs=1))
        ring = ctx.enter_context(tc.tile_pool(name="ring", bufs=1))
        psum = ctx.enter_context(tc.psum_pool(name="psum", bufs=1))
        ctx.enter_context(tc.manual_schedule())

        identity = keep.tile([P, P], F32, name="identity")
        make_identity(nc, identity[:])

        scales_first = keep.tile([P, 1, K], U8, name="scales_first", align_bytes=64)
        scales_rest = keep.tile([P, GROUPS - 1, K], U8, name="scales_rest", align_bytes=64)
        for scale_tile in (scales_first, scales_rest):
            nc.vector.memset(scale_tile[:].rearrange("p g n -> p (g n)").bitcast(I32), 0)
        c_scale_sb = [scales_first[:, 0, :]] + [scales_rest[:, i, :] for i in range(GROUPS - 1)]

        y_sb = [keep.tile([P, K], BF16, name="y_%d" % t, align_bytes=64) for t in range(TILES)]
        c_sb = [keep.tile([P, 2 * K], U8, name="c_%d" % g, align_bytes=64) for g in range(GROUPS)]
        back_sb = keep.tile([P, K], BF16, name="back_sb", align_bytes=64)

        def load_y(t, first=0, last=K):
            nc.sync.dma_start(out=y_sb[t][:, first:last], in_=y[t * P : (t + 1) * P, first:last])

        def load_c(g):
            nc.sync.dma_start(out=c_sb[g][:].bitcast(I32), in_=c_words[g].bitcast(I32))

        def load_scales(scale_tile, groups):
            for q in range(QUADRANTS):
                nc.sync.dma_start(
                    out=scale_tile[32 * q : 32 * q + 4, :, :].bitcast(I32),
                    in_=c_scales[groups, 4 * q : 4 * q + 4, :].bitcast(I32).rearrange("g r n -> r g n"),
                )

        load_y(0, 0, CHUNK)
        load_y(0, CHUNK, K)
        load_y(1)
        load_scales(scales_first, slice(0, 1))
        load_c(0)
        load_scales(scales_rest, slice(1, GROUPS))
        load_c(1)
        load_c(2)
        load_y(2)
        load_y(3)

        state = {(t, g): y_sb[t][:, g * CHUNK : (g + 1) * CHUNK] for t in range(TILES) for g in range(GROUPS)}
        sorted_pairs = {}
        operand = {}
        to_round = []
        to_quantize = []
        to_finish = []

        def sort_y(t, groups, copy):
            n = len(groups)
            pairs = keep.tile([P, n * PAIRS], F32, name="y_pairs_%d_%d" % (t, groups[0]), align_bytes=64)
            source = y_sb[t][:].bitcast(F32)[:, groups[0] * PAIRS : (groups[0] + n) * PAIRS]
            copy(
                out=pairs[:].rearrange("p (g u j) -> p g u j", g=n, u=2),
                in_=source.rearrange("p (g j u) -> p g u j", g=n, u=2),
            )
            for i, g in enumerate(groups):
                sorted_pairs[t, g] = pairs[:, i * PAIRS : (i + 1) * PAIRS]

        def round_states():
            for t, g in to_round:
                rounded = ring.tile([P, CHUNK], BF16, name="rounded", bufs=TILES * GROUPS, align_bytes=64)
                nc.scalar.copy(
                    out=rounded[:].rearrange("p (u j e) -> p u j e", u=2, e=2),
                    in_=state[t, g].rearrange("p (j u e) -> p u j e", u=2, e=2),
                )
                sorted_pairs[t, g] = rounded[:].bitcast(F32)
            to_round.clear()

        def turn(sweep, chunks_by_bank):
            banks = []
            for chunks in chunks_by_bank:
                bank = psum.tile([P, CHUNK], F32, name="turned", bufs=TURN_BANKS)
                for i, chunk in enumerate(chunks):
                    for u in range(2):
                        nc.tensor.transpose(
                            bank[:, (2 * i + u) * P : (2 * i + u + 1) * P],
                            sorted_pairs[chunk][:, u * P : (u + 1) * P],
                            identity[:],
                        )
                banks.append(bank)
            for chunks, bank in zip(chunks_by_bank, banks):
                n = len(chunks)
                grouped = ring.tile([P, n * PAIRS], F32, name="grouped", bufs=TURN_BANKS + 1, align_bytes=64)
                nc.scalar.copy(
                    out=grouped[:].rearrange("p (c r u) -> p c r u", c=n, u=2),
                    in_=bank[:, : n * PAIRS].rearrange("p (c u r) -> p c r u", c=n, u=2),
                )
                to_quantize.append((sweep, chunks, grouped))

        def quantize(count):
            for sweep, chunks, grouped in to_quantize[:count]:
                n = len(chunks)
                name = "%d_%d_%d" % (sweep, chunks[0][0], chunks[0][1])
                codes = keep.tile([P, n * P], U32, name="codes_" + name, align_bytes=64)
                scales = keep.tile([P, n * P], U8, name="scales_" + name, align_bytes=64)
                nc.vector.quantize_mx(out=codes[:].bitcast(FP8X4), scales=scales[:], in_=grouped[:].bitcast(BF16))
                for i, chunk in enumerate(chunks):
                    operand[chunk] = (codes[:, i * P : (i + 1) * P], scales[:, i * P : (i + 1) * P])
            to_quantize[:count] = []

        def turn_tile_pair(sweep, first):
            chunks = [(t, g) for t in (first, first + 1) for g in range(GROUPS)]
            turn(sweep, [chunks[i : i + 2] for i in range(0, len(chunks), 2)])
            quantize(2)

        def new_sum_bank():
            return psum.tile([P, CHUNK], F32, name="sums", bufs=SUM_BANKS)

        def mx_pass(sums, t, b, g):
            codes, scales = operand[t, g]
            nc.tensor.matmul_mx(
                out=sums[:],
                lhsT=codes.bitcast(FP8X4),
                lhsT_scale=scales,
                rhs=c_sb[g][:, 2 * b * CHUNK : 2 * (b + 1) * CHUNK].bitcast(FP4X4),
                rhs_scale=c_scale_sb[g][:, b * CHUNK : (b + 1) * CHUNK],
                start=(g == 0),
                stop=(g == GROUPS - 1),
            )

        def new_result():
            return ring.tile([P, CHUNK], F32, name="result", bufs=6)

        def times_back(engine, t, b, result, first, last):
            engine.tensor_tensor(
                out=result[:, first:last],
                in0=state[t, b][:, first:last],
                in1=back_sb[:, b * CHUNK + first : b * CHUNK + last],
                op=MULT,
            )

        def store(t, b, result, first, last):
            nc.sync.dma_start(
                out=out[t * P : (t + 1) * P, b * CHUNK + first : b * CHUNK + last], in_=result[:, first:last]
            )

        def add_residual(sweep, t, b, sums):
            if sweep < SWEEPS:
                new = keep.tile([P, CHUNK], F32, name="state_%d_%d_%d" % (sweep, t, b))
                to_round.append((t, b))
            else:
                new = ring.tile([P, CHUNK], F32, name="total", bufs=4)
            nc.vector.tensor_tensor(out=new[:], in0=sums[:], in1=state[t, b], op=ADD)
            state[t, b] = new[:]
            for earlier_t, earlier_b, result in to_finish:
                times_back(nc.vector, earlier_t, earlier_b, result, GPSIMD_COLUMNS, CHUNK)
                store(earlier_t, earlier_b, result, 0, CHUNK)
            to_finish.clear()
            quantize(len(to_quantize))

        def begin_product(t, b, transposes_follow):
            if (t, b) == (TILES - 1, GROUPS - 1):
                for first in (0, CHUNK // 2):
                    result = new_result()
                    times_back(nc.vector, t, b, result, first, first + CHUNK // 2)
                    store(t, b, result, first, first + CHUNK // 2)
            elif transposes_follow:
                result = new_result()
                times_back(nc.vector, t, b, result, 0, CHUNK)
                store(t, b, result, 0, CHUNK)
            else:
                result = new_result()
                times_back(nc.gpsimd, t, b, result, 0, GPSIMD_COLUMNS)
                to_finish.append((t, b, result))

        def sweep_tile(sweep, t, pair=None, turn_after=PASSES):
            for b in range(GROUPS):
                sums = new_sum_bank()
                for g in range(GROUPS):
                    mx_pass(sums, t, b, g)
                    if g == GROUPS - 1:
                        add_residual(sweep, t, b, sums)
                        if sweep == SWEEPS:
                            begin_product(t, b, bool(pair) and b == GROUPS - 1)
                    if pair and b * GROUPS + g + 1 == turn_after:
                        turn_tile_pair(*pair)
                if not pair or (b + 1) * GROUPS >= turn_after:
                    round_states()

        all_groups = list(range(GROUPS))

        for g in all_groups:
            sort_y(0, [g], nc.vector.tensor_copy)
        turn(1, [[(0, g)] for g in all_groups])
        for g in all_groups:
            sort_y(1, [g], nc.vector.tensor_copy)
        quantize(GROUPS)
        turn(1, [[(1, 0), (1, 1)], [(1, 2)]])
        quantize(2)

        first_sums = [new_sum_bank() for b in all_groups]
        for g in all_groups:
            for b in all_groups:
                mx_pass(first_sums[b], 0, b, g)
        sort_y(2, all_groups, nc.scalar.copy)
        sort_y(3, all_groups, nc.scalar.copy)
        for b in all_groups:
            round_states()
            add_residual(1, 0, b, first_sums[b])
        sweep_tile(1, 1, (1, 2), FIRST_TURN_AFTER)
        sweep_tile(1, 2, (2, 0))
        nc.scalar.dma_start(out=back_sb[:], in_=back.partition_broadcast(P))
        sweep_tile(1, 3)

        for sweep in range(2, SWEEPS + 1):
            sweep_tile(sweep, 0, (sweep, 2))
            sweep_tile(sweep, 1)
            sweep_tile(sweep, 2, (sweep + 1, 0) if sweep < SWEEPS else None)
            sweep_tile(sweep, 3)
